import numpy as np
import ml_dtypes


def mxq(x, axis, fmt="e4m3"):
    dtype, down = {"e4m3": (ml_dtypes.float8_e4m3fn, 7), "e5m2": (ml_dtypes.float8_e5m2, 14)}[fmt]
    v = np.moveaxis(np.asarray(x, np.float32).astype(ml_dtypes.bfloat16).astype(np.float64), axis, -1)
    blocks = v.reshape(v.shape[:-1] + (-1, 32))
    amax = np.abs(blocks).max(-1, keepdims=True)
    byte = np.maximum(np.where(amax > 0, np.frexp(amax)[1] - 1 + 127, 0) - down, 1)
    scale = np.exp2(byte - 127.0)
    codes = (blocks / scale).astype(np.float32).astype(dtype).astype(np.float64)
    return np.moveaxis((codes * scale).reshape(v.shape), -1, axis)


WIDE = False


def mx_kscale(k):
    if not WIDE:
        return np.ones(k)
    levels = np.array([10, -10, 5, -5, 0])
    if k % 512:
        return np.exp2(np.random.permutation(np.resize(levels, k // 32))).repeat(32)
    a = np.empty((k // 512, 16))
    for p in range(k // 512):
        a[p, :8] = np.random.permutation(np.resize(levels, 8))
        for g in range(8):
            far = levels[np.abs(levels - a[p, g]) >= 10]
            a[p, g + 8] = far[np.random.randint(len(far))]
    return np.exp2(a.ravel()).repeat(32)


def f64(x):
    return np.asarray(x).astype(np.float64)


def striped(idx):
    return np.tile(idx.reshape(-1, 16).T, (8, 1)).astype(np.uint16)


def unstriped(offs):
    return offs[:16].T.reshape(-1).astype(np.int64)


def striped8(idx):
    return np.concatenate([x.reshape(-1, 16).T for x in idx]).astype(np.uint16)


def runs(offs, k):
    lists = np.stack([offs[16 * r : 16 * r + 16].T.reshape(-1) for r in range(8)]).astype(np.int64)
    return lists[np.arange(k) % 512 // 64]


def pack_weight(w):
    k, n = w.shape
    w = f64(np.asarray(w, np.float32).astype(ml_dtypes.bfloat16)).reshape(k // 32, 32, n)
    amax = np.abs(w).max(1)
    byte = np.clip(np.where(amax > 0, np.frexp(amax)[1] - 1 + 127 - 7, 1), 1, 254)
    scaled = (w * np.exp2(127.0 - byte)[:, None, :]).reshape(k, n).astype(np.float32)
    words = np.ascontiguousarray(scaled.reshape(k // 512, 128, 4, n).transpose(0, 1, 3, 2)).astype(ml_dtypes.float8_e4m3fn).view(np.uint8)
    return words, np.ascontiguousarray(byte.astype(np.uint8).reshape(k // 512, 16, n))


def unpack_weight(words, scales):
    g, p, n, _ = words.shape
    vals = np.ascontiguousarray(words).view(ml_dtypes.float8_e4m3fn).astype(np.float64) * np.repeat(np.exp2(scales.astype(np.float64) - 127.0), 8, axis=1)[..., None]
    return vals.transpose(0, 1, 3, 2).reshape(g * 512, n)


def sigmoid(v):
    return 1.0 / (1.0 + np.exp(-np.maximum(v, -700.0)))


K, T, S, N, H = 512, 2048, 512, 512, 512


def setup_inputs():
    n = np.random.standard_normal
    s = mx_kscale(K)[:, None]
    u = mx_kscale(H)
    packed_xT = pack_weight(n((K, T)) * s)
    return {
        "x_words": packed_xT[0],
        "x_scales": packed_xT[1],
        "w1": (n((K, H)) / np.sqrt(K) / s).astype(np.float32),
        "gn": (np.random.uniform(0.5, 1.5, (H, 1)) * u[:, None]).astype(np.float32),
        "w2": (n((H, N)) / np.sqrt(H) / u[:, None]).astype(np.float32),
        "gm": (np.random.uniform(0.5, 1.5, (H, 1)) * u[:, None]).astype(np.float32),
        "w3": (n((H, N)) / np.sqrt(H) / u[:, None]).astype(np.float32),
        "offs": striped(np.random.permutation(T)[:S]),
        "n1": striped8(np.stack([np.random.permutation(S) for _ in range(8)])),
        "n2": striped8(np.stack([np.random.permutation(S) for _ in range(8)])),
        "n3": striped8(np.stack([np.random.permutation(S) for _ in range(8)])),
        "n4": striped8(np.stack([np.random.permutation(S) for _ in range(8)])),
        "n5": striped8(np.stack([np.random.permutation(S) for _ in range(8)])),
        "n6": striped8(np.stack([np.random.permutation(S) for _ in range(8)])),
    }


def reference(x_words, x_scales, w1, gn, w2, gm, w3, offs, n1, n2, n3, n4, n5, n6):
    xq = unpack_weight(x_words, x_scales)[:, unstriped(offs)]
    y = mxq(f64(w1), 0, "e4m3").T @ xq
    z = f64(gn) * (0.75 * ((y - (y[np.arange(H)[:, None], runs(n1, H)])) * (y - (y[np.arange(H)[:, None], runs(n2, H)]))))
    a = mxq(f64(w2), 0, "e4m3").T @ mxq(z, 0, "e4m3")
    z2 = f64(gm) * ((np.tanh(y[np.arange(H)[:, None], runs(n3, H)] - y)) * (y[np.arange(H)[:, None], runs(n4, H)]))
    b = mxq(f64(w3), 0, "e4m3").T @ mxq(z2, 0, "e4m3")
    return a + (sigmoid(b[np.arange(N)[:, None], runs(n6, N)] - b)) * (a[np.arange(N)[:, None], runs(n5, N)] - a)

@@ -1,0 +1,196 @@
+from contextlib import ExitStack
+
+import concourse.mybir as mybir
+
+K, T, S, H, N = 512, 2048, 512, 512, 512
+FLOPS = 2 * S * (K * H + 2 * H * N)
+
+F32 = mybir.dt.float32
+BF16 = mybir.dt.bfloat16
+I32 = mybir.dt.int32
+U32 = mybir.dt.uint32
+U16 = mybir.dt.uint16
+U8 = mybir.dt.uint8
+FP8X4 = mybir.dt.float8_e4m3fn_x4
+ALU = mybir.AluOpType
+ACT = mybir.ActivationFunctionType
+
+P = 128
+PACK = 4
+WIN = 2 * S
+
+
+def tile_picked_forkpullbquadfdif_none_p_kernel(tc, x_words, x_scales, w1, gn, w2, gm, w3, offs, n1, n2, n3, n4, n5, n6, out):
+    nc = tc.nc
+    with ExitStack() as ctx:
+        keep = ctx.enter_context(tc.tile_pool(name="keep", bufs=1))
+        psum = ctx.enter_context(tc.psum_pool(name="psum", bufs=1))
+
+        def sb(name, shape, dtype):
+            return keep.tile(shape, dtype, name=name, align_bytes=64)
+
+        lists = {}
+
+        def load_list(name, src):
+            lists[name] = sb("list_" + name, [P, S // 16], U16)
+            nc.sync.dma_start(lists[name][:], src)
+
+        xs_all = sb("xs_all", [P, T], U8)
+        nc.vector.memset(xs_all[:].bitcast(I32), 0)
+        for q in range(4):
+            nc.scalar.dma_start(xs_all[32 * q : 32 * q + 4, :].bitcast(I32), x_scales[0, 4 * q : 4 * q + 4, :].bitcast(I32))
+        load_list("offs", offs)
+        xw_all = sb("xw_all", [P, T], I32)
+        nc.sync.dma_start(xw_all[:], x_words[0].rearrange("p n t -> p (n t)").bitcast(I32))
+        w1_rows = w1.rearrange("(p j) c -> p j c", j=PACK)
+        w1_raw = [sb("w1_raw%d" % u, [P, PACK, H // 2], F32) for u in range(2)]
+        for u in range(2):
+            nc.sync.dma_start(w1_raw[u][:], w1_rows[:, :, u * (H // 2) : (u + 1) * (H // 2)])
+        gn_sb = sb("gn_sb", [P, PACK], F32)
+        gm_sb = sb("gm_sb", [P, PACK], F32)
+        nc.gpsimd.dma_start(gn_sb[:], gn.rearrange("(p t) o -> p (t o)", t=PACK))
+        nc.gpsimd.dma_start(gm_sb[:], gm.rearrange("(p t) o -> p (t o)", t=PACK))
+        load_list("n3", n3)
+        load_list("n1", n1)
+        load_list("n2", n2)
+        w2_raw = sb("w2_raw", [P, PACK, N], F32)
+        nc.sync.dma_start(w2_raw[:], w2.rearrange("(p j) c -> p j c", j=PACK))
+        w3_raw = sb("w3_raw", [P, PACK, N], F32)
+        nc.sync.dma_start(w3_raw[:], w3.rearrange("(p j) c -> p j c", j=PACK))
+        load_list("n4", n4)
+        load_list("n5", n5)
+        load_list("n6", n6)
+
+        warm = sb("warm", [P, 1], F32)
+        nc.gpsimd.memset(warm[:], 0.0)
+        nc.scalar.activation(warm[:], warm[:], ACT.Tanh)
+
+        win_a = [sb("win_a%d" % t, [P, WIN], F32) for t in range(PACK)]
+        win_b = [sb("win_b%d" % t, [P, WIN], F32) for t in range(PACK)]
+        for t in range(PACK):
+            nc.gpsimd.memset(win_a[t][:, S:], 0.0)
+
+        xs = sb("xs", [P, S], U8)
+        xw = sb("xw", [P, S], U32)
+        nc.vector.tensor_copy(xs[:], xs_all[:].indirect(lists["offs"][:]))
+        nc.vector.tensor_copy(xw[:], xw_all[:].bitcast(U32).indirect(lists["offs"][:]))
+
+        def dealt(grouped):
+            return grouped[:].rearrange("p (t m j) -> p m j t", t=PACK, j=PACK)
+
+        def by_line(raw):
+            return raw[:].rearrange("p j (m t) -> p m j t", t=PACK)
+
+        w1_bf = sb("w1_bf", [P, PACK * H], BF16)
+        nc.scalar.copy(dealt(w1_bf)[:, 0:64], by_line(w1_raw[0]))
+        nc.vector.tensor_copy(dealt(w1_bf)[:, 64:128], by_line(w1_raw[1]))
+        w1_codes = sb("w1_codes", [P, H], U32)
+        w1_sc = sb("w1_sc", [P, H], U8)
+
+        bank_yb = [psum.tile([P, S], F32, name="bank_yb%d" % t) for t in range(PACK)]
+        bank_a = [psum.tile([P, S], F32, name="bank_a%d" % t) for t in range(PACK)]
+
+        def product(bank, w_codes, w_sc, t, codes, sc):
+            cols = slice(t * P, (t + 1) * P)
+            nc.tensor.matmul_mx(out=bank[:], lhsT=w_codes[:, cols].bitcast(FP8X4), lhsT_scale=w_sc[:, cols],
+                                rhs=codes[:].bitcast(FP8X4), rhs_scale=sc[:], start=True, stop=True)
+
+        for t in range(PACK):
+            cols = slice(t * P, (t + 1) * P)
+            nc.vector.quantize_mx(out=w1_codes[:, cols].bitcast(FP8X4), scales=w1_sc[:, cols], in_=w1_bf[:, t * H : (t + 1) * H])
+            product(bank_yb[t], w1_codes, w1_sc, t, xw, xs)
+
+        for t in range(PACK):
+            nc.scalar.copy(win_a[t][:, :S], bank_yb[t][:])
+            nc.scalar.copy(win_b[t][:, S:], bank_yb[t][:])
+
+        d1 = [sb("d1_%d" % t, [P, S], F32) for t in range(PACK)]
+        d2 = [sb("d2_%d" % t, [P, S], F32) for t in range(PACK)]
+        d3 = [sb("d3_%d" % t, [P, S], F32) for t in range(PACK)]
+        th = [sb("th_%d" % t, [P, S], F32) for t in range(PACK)]
+        zf = sb("zf", [P, PACK, S], F32)
+        z2f = sb("z2f", [P, PACK, S], F32)
+
+        def diff(dst, win, name, plain):
+            nc.vector.tensor_tensor(dst, win[:].indirect(lists[name][:]), plain, ALU.subtract)
+
+        def z_product(t):
+            nc.vector.scalar_tensor_tensor(zf[:, t, :], d1[t][:], gn_sb[:, t : t + 1], d2[t][:], ALU.mult, ALU.mult)
+
+        def cast_weight(name, raw):
+            w_bf = sb(name + "_bf", [P, PACK * N], BF16)
+            nc.scalar.copy(dealt(w_bf), by_line(raw))
+            return w_bf
+
+        def quantise(name, src):
+            codes = sb(name + "_codes", [P, S], U32)
+            sc = sb(name + "_sc", [P, S], U8)
+            nc.vector.quantize_mx(out=codes[:].bitcast(FP8X4), scales=sc[:], in_=src[:])
+            return codes, sc
+
+        def interleave(name, src, scale):
+            z_bf = sb(name + "_bf", [P, PACK * S], BF16)
+            nc.scalar.activation(z_bf[:].rearrange("p (c i t) -> p c t i", i=4, t=PACK),
+                                 src[:].rearrange("p t (c i) -> p c t i", i=4), ACT.Copy, scale=scale)
+            return z_bf
+
+        for t in range(PACK):
+            y_plain = win_b[t][:, S:]
+            diff(d3[t][:], win_a[t], "n3", y_plain)
+            if t > 0:
+                z_product(t - 1)
+            diff(d1[t][:], win_a[t], "n1", y_plain)
+            diff(d2[t][:], win_a[t], "n2", y_plain)
+            nc.scalar.activation(th[t][:], d3[t][:], ACT.Tanh)
+            nc.scalar.activation(win_b[t][:, :S], bank_yb[t][:], ACT.Copy, scale=gm_sb[:, t : t + 1])
+            if t == 0:
+                w2_bf = cast_weight("w2", w2_raw)
+            if t == 1:
+                w3_bf = cast_weight("w3", w3_raw)
+            if t == 2:
+                w2_codes, w2_sc = quantise("w2", w2_bf)
+            if t == 3:
+                w3_codes, w3_sc = quantise("w3", w3_bf)
+
+        def z2_product(t):
+            nc.vector.tensor_tensor(z2f[:, t, :], win_b[t][:].indirect(lists["n4"][:]), th[t][:], ALU.mult)
+
+        z_product(PACK - 1)
+        z_bf = interleave("z", zf, 0.75)
+        z2_product(0)
+        z2_product(1)
+        z2_product(2)
+        z_codes, z_sc = quantise("z", z_bf)
+        a_plain = [sb("a_plain%d" % t, [P, S], F32) for t in range(PACK)]
+        for t in range(PACK):
+            product(bank_a[t], w2_codes, w2_sc, t, z_codes, z_sc)
+        z2_product(3)
+        nc.scalar.copy(win_a[0][:, :S], bank_a[0][:])
+        nc.scalar.copy(a_plain[0][:], bank_a[0][:])
+        z2_bf = interleave("z2", z2f, 1.0)
+        for t in range(1, PACK):
+            nc.scalar.copy(win_a[t][:, :S], bank_a[t][:])
+            nc.scalar.copy(a_plain[t][:], bank_a[t][:])
+        for t in range(PACK):
+            diff(d1[t][:], win_a[t], "n5", a_plain[t][:])
+            if t == 1:
+                z2_codes, z2_sc = quantise("z2", z2_bf)
+        for t in range(PACK):
+            product(bank_yb[t], w3_codes, w3_sc, t, z2_codes, z2_sc)
+        for t in range(PACK):
+            nc.scalar.copy(win_b[t][:, :S], bank_yb[t][:])
+            nc.scalar.copy(d2[t][:], bank_yb[t][:])
+
+        out_rows = out.rearrange("(p t) j -> p t j", t=PACK)
+
+        def finish(t):
+            nc.vector.scalar_tensor_tensor(d3[t][:], th[t][:], 1.0, d1[t][:], ALU.add, ALU.mult)
+            nc.vector.scalar_tensor_tensor(zf[:, t, :], d3[t][:], 0.5, a_plain[t][:], ALU.mult, ALU.add)
+            nc.sync.dma_start(out_rows[:, t, :], zf[:, t, :])
+
+        for t in range(PACK):
+            diff(d3[t][:], win_b[t], "n6", d2[t][:])
+            nc.scalar.activation(th[t][:], d3[t][:], ACT.Tanh, scale=0.5)
+            if t > 0:
+                finish(t - 1)
+        finish(PACK - 1)

@@ -36,23 +36,24 @@ def tile_picked_forkpullbquadfdif_none_p_kernel(tc, x_words, x_scales, w1, gn, w
             nc.sync.dma_start(lists[name][:], src)
 
         xs_all = sb("xs_all", [P, T], U8)
-        nc.vector.memset(xs_all[:].bitcast(I32), 0)
-        for q in range(4):
-            nc.scalar.dma_start(xs_all[32 * q : 32 * q + 4, :].bitcast(I32), x_scales[0, 4 * q : 4 * q + 4, :].bitcast(I32))
+        nc.gpsimd.memset(xs_all[:, : T // 2].bitcast(I32), 0)
+        nc.vector.memset(xs_all[:, T // 2 :].bitcast(I32), 0)
+        gn_raw = keep.tile([P, PACK], F32, name="gn_raw", tag="gn_then_words", align_bytes=64)
+        nc.sync.dma_start(gn_raw[:], gn.rearrange("(p t) o -> p (t o)", t=PACK))
         load_list("offs", offs)
-        xw_all = sb("xw_all", [P, T], I32)
-        nc.sync.dma_start(xw_all[:], x_words[0].rearrange("p n t -> p (n t)").bitcast(I32))
-        w1_rows = w1.rearrange("(p j) c -> p j c", j=PACK)
-        w1_raw = [sb("w1_raw%d" % u, [P, PACK, H // 2], F32) for u in range(2)]
-        for u in range(2):
-            nc.sync.dma_start(w1_raw[u][:], w1_rows[:, :, u * (H // 2) : (u + 1) * (H // 2)])
+        w1_raw = sb("w1_raw", [P, PACK, H], F32)
+        nc.sync.dma_start(w1_raw[:], w1.rearrange("(p j) c -> p j c", j=PACK))
+        for q in range(4):
+            nc.sync.dma_start(xs_all[32 * q : 32 * q + 4, :].bitcast(I32), x_scales[0, 4 * q : 4 * q + 4, :].bitcast(I32))
         gn_sb = sb("gn_sb", [P, PACK], F32)
-        gm_sb = sb("gm_sb", [P, PACK], F32)
-        nc.gpsimd.dma_start(gn_sb[:], gn.rearrange("(p t) o -> p (t o)", t=PACK))
-        nc.gpsimd.dma_start(gm_sb[:], gm.rearrange("(p t) o -> p (t o)", t=PACK))
-        load_list("n3", n3)
+        nc.vector.tensor_scalar_mul(gn_sb[:], gn_raw[:], 0.75)
+        xw_all = keep.tile([P, T], I32, name="xw_all", tag="gn_then_words", align_bytes=64)
+        nc.sync.dma_start(xw_all[:], x_words[0].rearrange("p n t -> p (n t)").bitcast(I32))
         load_list("n1", n1)
         load_list("n2", n2)
+        gm_sb = sb("gm_sb", [P, PACK], F32)
+        load_list("n3", n3)
+        nc.sync.dma_start(gm_sb[:], gm.rearrange("(p t) o -> p (t o)", t=PACK))
         w2_raw = sb("w2_raw", [P, PACK, N], F32)
         nc.sync.dma_start(w2_raw[:], w2.rearrange("(p j) c -> p j c", j=PACK))
         w3_raw = sb("w3_raw", [P, PACK, N], F32)
@@ -61,19 +62,16 @@ def tile_picked_forkpullbquadfdif_none_p_kernel(tc, x_words, x_scales, w1, gn, w
         load_list("n5", n5)
         load_list("n6", n6)
 
-        warm = sb("warm", [P, 1], F32)
-        nc.gpsimd.memset(warm[:], 0.0)
-        nc.scalar.activation(warm[:], warm[:], ACT.Tanh)
 
         win_a = [sb("win_a%d" % t, [P, WIN], F32) for t in range(PACK)]
         win_b = [sb("win_b%d" % t, [P, WIN], F32) for t in range(PACK)]
         for t in range(PACK):
-            nc.gpsimd.memset(win_a[t][:, S:], 0.0)
+            nc.vector.memset(win_a[t][:, S:], 0.0)
 
+        lo_half, hi_half = slice(0, S // 2), slice(S // 2, S)
         xs = sb("xs", [P, S], U8)
-        xw = sb("xw", [P, S], U32)
+        xw = [sb("xw%d" % h, [P, S // 2], U32) for h in range(2)]
         nc.vector.tensor_copy(xs[:], xs_all[:].indirect(lists["offs"][:]))
-        nc.vector.tensor_copy(xw[:], xw_all[:].bitcast(U32).indirect(lists["offs"][:]))
 
         def dealt(grouped):
             return grouped[:].rearrange("p (t m j) -> p m j t", t=PACK, j=PACK)
@@ -82,37 +80,53 @@ def tile_picked_forkpullbquadfdif_none_p_kernel(tc, x_words, x_scales, w1, gn, w
             return raw[:].rearrange("p j (m t) -> p m j t", t=PACK)
 
         w1_bf = sb("w1_bf", [P, PACK * H], BF16)
-        nc.scalar.copy(dealt(w1_bf)[:, 0:64], by_line(w1_raw[0]))
-        nc.vector.tensor_copy(dealt(w1_bf)[:, 64:128], by_line(w1_raw[1]))
+        nc.scalar.copy(dealt(w1_bf)[:, 0:64], by_line(w1_raw)[:, 0:64])
+        nc.vector.tensor_copy(dealt(w1_bf)[:, 64:128], by_line(w1_raw)[:, 64:128])
         w1_codes = sb("w1_codes", [P, H], U32)
         w1_sc = sb("w1_sc", [P, H], U8)
 
         bank_yb = [psum.tile([P, S], F32, name="bank_yb%d" % t) for t in range(PACK)]
         bank_a = [psum.tile([P, S], F32, name="bank_a%d" % t) for t in range(PACK)]
 
-        def product(bank, w_codes, w_sc, t, codes, sc):
+        def product(dst, w_codes, w_sc, t, codes, sc):
             cols = slice(t * P, (t + 1) * P)
-            nc.tensor.matmul_mx(out=bank[:], lhsT=w_codes[:, cols].bitcast(FP8X4), lhsT_scale=w_sc[:, cols],
-                                rhs=codes[:].bitcast(FP8X4), rhs_scale=sc[:], start=True, stop=True)
+            nc.tensor.matmul_mx(out=dst, lhsT=w_codes[:, cols].bitcast(FP8X4), lhsT_scale=w_sc[:, cols],
+                                rhs=codes.bitcast(FP8X4), rhs_scale=sc, start=True, stop=True)
 
-        for t in range(PACK):
-            cols = slice(t * P, (t + 1) * P)
-            nc.vector.quantize_mx(out=w1_codes[:, cols].bitcast(FP8X4), scales=w1_sc[:, cols], in_=w1_bf[:, t * H : (t + 1) * H])
-            product(bank_yb[t], w1_codes, w1_sc, t, xw, xs)
+        spare_bank = bank_a[PACK - 1]
 
-        for t in range(PACK):
+        nc.vector.quantize_mx(out=w1_codes[:].bitcast(FP8X4), scales=w1_sc[:], in_=w1_bf[:])
+        nc.vector.tensor_copy(xw[0][:], xw_all[:].bitcast(U32).indirect(lists["offs"][:, 0:16]))
+        nc.vector.tensor_copy(xw[1][:], xw_all[:].bitcast(U32).indirect(lists["offs"][:, 16:32]))
+        product(bank_yb[0][:, lo_half], w1_codes, w1_sc, 0, xw[0][:], xs[:, lo_half])
+        product(spare_bank[:, hi_half], w1_codes, w1_sc, 0, xw[1][:], xs[:, hi_half])
+        for t in range(1, PACK):
+            product(bank_yb[t][:, lo_half], w1_codes, w1_sc, t, xw[0][:], xs[:, lo_half])
+            product(bank_yb[t][:, hi_half], w1_codes, w1_sc, t, xw[1][:], xs[:, hi_half])
+
+        nc.scalar.copy(win_a[0][:, lo_half], bank_yb[0][:, lo_half])
+        nc.vector.tensor_copy(win_b[0][:, S : S + S // 2], bank_yb[0][:, lo_half])
+        nc.scalar.copy(win_a[0][:, hi_half], spare_bank[:, hi_half])
+        nc.scalar.copy(win_b[0][:, S + S // 2 :], spare_bank[:, hi_half])
+        for t in range(1, PACK):
             nc.scalar.copy(win_a[t][:, :S], bank_yb[t][:])
             nc.scalar.copy(win_b[t][:, S:], bank_yb[t][:])
 
         d1 = [sb("d1_%d" % t, [P, S], F32) for t in range(PACK)]
         d2 = [sb("d2_%d" % t, [P, S], F32) for t in range(PACK)]
-        d3 = [sb("d3_%d" % t, [P, S], F32) for t in range(PACK)]
+        z_bf = sb("z_bf", [P, PACK * S], BF16)
+        z2_bf = sb("z2_bf", [P, PACK * S], BF16)
+        d3 = [d1[2][:], d1[3][:], d2[3][:], z_bf[:, S : 3 * S].bitcast(F32)]
+        d5 = [d1[0][:], d1[1][:], z2_bf[:, : 2 * S].bitcast(F32), z2_bf[:, 2 * S :].bitcast(F32)]
+        d6 = [sb("d6_%d" % t, [P, S], F32) for t in range(PACK)]
         th = [sb("th_%d" % t, [P, S], F32) for t in range(PACK)]
         zf = sb("zf", [P, PACK, S], F32)
-        z2f = sb("z2f", [P, PACK, S], F32)
+        z2f_lo = sb("z2f_lo", [P, PACK * S // 2], F32)
+        z2f = [z2f_lo[:].rearrange("p (t c) -> p t c", t=PACK), z_bf[:].bitcast(F32).rearrange("p (t c) -> p t c", t=PACK)]
+        halves = [lo_half, hi_half]
 
-        def diff(dst, win, name, plain):
-            nc.vector.tensor_tensor(dst, win[:].indirect(lists[name][:]), plain, ALU.subtract)
+        def diff(dst, win, offsets, plain):
+            nc.vector.tensor_tensor(dst, win[:].indirect(offsets), plain, ALU.subtract)
 
         def z_product(t):
             nc.vector.scalar_tensor_tensor(zf[:, t, :], d1[t][:], gn_sb[:, t : t + 1], d2[t][:], ALU.mult, ALU.mult)
@@ -128,69 +142,84 @@ def tile_picked_forkpullbquadfdif_none_p_kernel(tc, x_words, x_scales, w1, gn, w
             nc.vector.quantize_mx(out=codes[:].bitcast(FP8X4), scales=sc[:], in_=src[:])
             return codes, sc
 
-        def interleave(name, src, scale):
-            z_bf = sb(name + "_bf", [P, PACK * S], BF16)
-            nc.scalar.activation(z_bf[:].rearrange("p (c i t) -> p c t i", i=4, t=PACK),
-                                 src[:].rearrange("p t (c i) -> p c t i", i=4), ACT.Copy, scale=scale)
-            return z_bf
+        def interleave(dst, src):
+            nc.scalar.copy(dst.rearrange("p (c i t) -> p c t i", i=4, t=PACK),
+                           src.rearrange("p t (c i) -> p c t i", i=4))
 
+        y_plain = [win_b[t][:, S:] for t in range(PACK)]
         for t in range(PACK):
-            y_plain = win_b[t][:, S:]
-            diff(d3[t][:], win_a[t], "n3", y_plain)
-            if t > 0:
-                z_product(t - 1)
-            diff(d1[t][:], win_a[t], "n1", y_plain)
-            diff(d2[t][:], win_a[t], "n2", y_plain)
-            nc.scalar.activation(th[t][:], d3[t][:], ACT.Tanh)
-            nc.scalar.activation(win_b[t][:, :S], bank_yb[t][:], ACT.Copy, scale=gm_sb[:, t : t + 1])
             if t == 0:
-                w2_bf = cast_weight("w2", w2_raw)
-            if t == 1:
-                w3_bf = cast_weight("w3", w3_raw)
-            if t == 2:
-                w2_codes, w2_sc = quantise("w2", w2_bf)
-            if t == 3:
-                w3_codes, w3_sc = quantise("w3", w3_bf)
-
-        def z2_product(t):
-            nc.vector.tensor_tensor(z2f[:, t, :], win_b[t][:].indirect(lists["n4"][:]), th[t][:], ALU.mult)
-
+                diff(d1[0][:, lo_half], win_a[0], lists["n1"][:, 0:16], y_plain[0][:, lo_half])
+                diff(d1[0][:, hi_half], win_a[0], lists["n1"][:, 16:32], y_plain[0][:, hi_half])
+            else:
+                diff(d1[t][:], win_a[t], lists["n1"][:], y_plain[t])
+                z_product(t - 1)
+            diff(d2[t][:], win_a[t], lists["n2"][:], y_plain[t])
+        w2_bf = cast_weight("w2", w2_raw)
+        w2_codes, w2_sc = quantise("w2", w2_bf)
+        for t in range(PACK):
+            nc.scalar.activation(win_b[t][:, :S], win_a[t][:, :S], ACT.Copy, scale=gm_sb[:, t : t + 1])
+        w3_bf = cast_weight("w3", w3_raw)
         z_product(PACK - 1)
-        z_bf = interleave("z", zf, 0.75)
-        z2_product(0)
-        z2_product(1)
-        z2_product(2)
+        interleave(z_bf[:], zf[:])
+
+        def tanh_diff(t):
+            diff(d3[t], win_a[t], lists["n3"][:], y_plain[t])
+            nc.scalar.activation(th[t][:], d3[t], ACT.Tanh)
+
+        tanh_diff(0)
+        tanh_diff(1)
+        tanh_diff(2)
         z_codes, z_sc = quantise("z", z_bf)
+        tanh_diff(3)
+        w3_codes, w3_sc = quantise("w3", w3_bf)
         a_plain = [sb("a_plain%d" % t, [P, S], F32) for t in range(PACK)]
         for t in range(PACK):
-            product(bank_a[t], w2_codes, w2_sc, t, z_codes, z_sc)
-        z2_product(3)
-        nc.scalar.copy(win_a[0][:, :S], bank_a[0][:])
-        nc.scalar.copy(a_plain[0][:], bank_a[0][:])
-        z2_bf = interleave("z2", z2f, 1.0)
-        for t in range(1, PACK):
+            product(bank_a[t][:], w2_codes, w2_sc, t, z_codes[:], z_sc[:])
+        for h in range(2):
+            for t in range(PACK):
+                nc.vector.tensor_tensor(z2f[h][:, t, :], win_b[t][:].indirect(lists["n4"][:, 16 * h : 16 * h + 16]), th[t][:, halves[h]], ALU.mult)
+        for t in range(PACK):
             nc.scalar.copy(win_a[t][:, :S], bank_a[t][:])
             nc.scalar.copy(a_plain[t][:], bank_a[t][:])
+        for h in range(2):
+            interleave(z2_bf[:, 2 * S * h : 2 * S * (h + 1)], z2f[h])
         for t in range(PACK):
-            diff(d1[t][:], win_a[t], "n5", a_plain[t][:])
+            diff(d5[t], win_a[t], lists["n5"][:], a_plain[t][:])
             if t == 1:
                 z2_codes, z2_sc = quantise("z2", z2_bf)
         for t in range(PACK):
-            product(bank_yb[t], w3_codes, w3_sc, t, z2_codes, z2_sc)
+            product(bank_yb[t][:], w3_codes, w3_sc, t, z2_codes[:], z2_sc[:])
+        b_plain = [sb("b_plain%d" % t, [P, S], F32) for t in range(PACK)]
         for t in range(PACK):
             nc.scalar.copy(win_b[t][:, :S], bank_yb[t][:])
-            nc.scalar.copy(d2[t][:], bank_yb[t][:])
+            nc.scalar.copy(b_plain[t][:], bank_yb[t][:])
+
 
         out_rows = out.rearrange("(p t) j -> p t j", t=PACK)
 
-        def finish(t):
-            nc.vector.scalar_tensor_tensor(d3[t][:], th[t][:], 1.0, d1[t][:], ALU.add, ALU.mult)
-            nc.vector.scalar_tensor_tensor(zf[:, t, :], d3[t][:], 0.5, a_plain[t][:], ALU.mult, ALU.add)
-            nc.sync.dma_start(out_rows[:, t, :], zf[:, t, :])
+        def gate(t):
+            diff(d6[t][:], win_b[t], lists["n6"][:], b_plain[t][:])
+            nc.scalar.activation(th[t][:], d6[t][:], ACT.Tanh, scale=0.5)
 
-        for t in range(PACK):
-            diff(d3[t][:], win_b[t], "n6", d2[t][:])
-            nc.scalar.activation(th[t][:], d3[t][:], ACT.Tanh, scale=0.5)
-            if t > 0:
-                finish(t - 1)
-        finish(PACK - 1)
+        def pull(t, tok=slice(0, S)):
+            nc.vector.scalar_tensor_tensor(d6[t][:, tok], th[t][:, tok], 1.0, d5[t][:, tok], ALU.add, ALU.mult)
+
+        def finish(t, tok=slice(0, S)):
+            nc.vector.scalar_tensor_tensor(zf[:, t, tok], d6[t][:, tok], 0.5, a_plain[t][:, tok], ALU.mult, ALU.add)
+            nc.sync.dma_start(out_rows[:, t, tok], zf[:, t, tok])
+
+        gate(0)
+        gate(1)
+        pull(0)
+        gate(2)
+        finish(0)
+        pull(1)
+        gate(3)
+        finish(1)
+        pull(2)
+        pull(3, lo_half)
+        finish(2)
+        pull(3, hi_half)
+        finish(3, lo_half)
+        finish(3, hi_half)

@@ -36,15 +36,15 @@ def tile_picked_forkpullbquadfdif_none_p_kernel(tc, x_words, x_scales, w1, gn, w
             nc.sync.dma_start(lists[name][:], src)
 
         xs_all = sb("xs_all", [P, T], U8)
-        nc.gpsimd.memset(xs_all[:, : T // 2].bitcast(I32), 0)
-        nc.vector.memset(xs_all[:, T // 2 :].bitcast(I32), 0)
+        nc.gpsimd.memset(xs_all[:, : 3 * T // 4].bitcast(I32), 0)
+        nc.vector.memset(xs_all[:, 3 * T // 4 :].bitcast(I32), 0)
         gn_raw = keep.tile([P, PACK], F32, name="gn_raw", tag="gn_then_words", align_bytes=64)
         nc.sync.dma_start(gn_raw[:], gn.rearrange("(p t) o -> p (t o)", t=PACK))
         load_list("offs", offs)
         w1_raw = sb("w1_raw", [P, PACK, H], F32)
         nc.sync.dma_start(w1_raw[:], w1.rearrange("(p j) c -> p j c", j=PACK))
         for q in range(4):
-            nc.sync.dma_start(xs_all[32 * q : 32 * q + 4, :].bitcast(I32), x_scales[0, 4 * q : 4 * q + 4, :].bitcast(I32))
+            nc.sync.dma_start(xs_all[q:P:32, :].bitcast(I32), x_scales[0, q:16:4, :].bitcast(I32))
         gn_sb = sb("gn_sb", [P, PACK], F32)
         nc.vector.tensor_scalar_mul(gn_sb[:], gn_raw[:], 0.75)
         xw_all = keep.tile([P, T], I32, name="xw_all", tag="gn_then_words", align_bytes=64)
@@ -80,8 +80,8 @@ def tile_picked_forkpullbquadfdif_none_p_kernel(tc, x_words, x_scales, w1, gn, w
             return raw[:].rearrange("p j (m t) -> p m j t", t=PACK)
 
         w1_bf = sb("w1_bf", [P, PACK * H], BF16)
-        nc.scalar.copy(dealt(w1_bf)[:, 0:64], by_line(w1_raw)[:, 0:64])
-        nc.vector.tensor_copy(dealt(w1_bf)[:, 64:128], by_line(w1_raw)[:, 64:128])
+        nc.scalar.copy(dealt(w1_bf)[:, 0:96], by_line(w1_raw)[:, 0:96])
+        nc.vector.tensor_copy(dealt(w1_bf)[:, 96:128], by_line(w1_raw)[:, 96:128])
         w1_codes = sb("w1_codes", [P, H], U32)
         w1_sc = sb("w1_sc", [P, H], U8)
 
@@ -116,13 +116,15 @@ def tile_picked_forkpullbquadfdif_none_p_kernel(tc, x_words, x_scales, w1, gn, w
         d2 = [sb("d2_%d" % t, [P, S], F32) for t in range(PACK)]
         z_bf = sb("z_bf", [P, PACK * S], BF16)
         z2_bf = sb("z2_bf", [P, PACK * S], BF16)
-        d3 = [d1[2][:], d1[3][:], d2[3][:], z_bf[:, S : 3 * S].bitcast(F32)]
-        d5 = [d1[0][:], d1[1][:], z2_bf[:, : 2 * S].bitcast(F32), z2_bf[:, 2 * S :].bitcast(F32)]
+        zf_flat = sb("zf", [P, PACK * S], F32)
+        zf = zf_flat[:].rearrange("p (t c) -> p t c", t=PACK)
+        res = [sb("res%d" % t, [P, S], F32) for t in range(PACK)]
+        d3 = [d1[2][:], d1[3][:], d2[3][:], zf_flat[:, S // 2 : 3 * S // 2]]
+        d5 = [d1[0][:], d1[1][:], zf_flat[:, :S], zf_flat[:, S : 2 * S]]
         d6 = [sb("d6_%d" % t, [P, S], F32) for t in range(PACK)]
         th = [sb("th_%d" % t, [P, S], F32) for t in range(PACK)]
-        zf = sb("zf", [P, PACK, S], F32)
         z2f_lo = sb("z2f_lo", [P, PACK * S // 2], F32)
-        z2f = [z2f_lo[:].rearrange("p (t c) -> p t c", t=PACK), z_bf[:].bitcast(F32).rearrange("p (t c) -> p t c", t=PACK)]
+        z2f = [z2f_lo[:].rearrange("p (t c) -> p t c", t=PACK), zf_flat[:, : 2 * S].rearrange("p (t c) -> p t c", t=PACK)]
         halves = [lo_half, hi_half]
 
         def diff(dst, win, offsets, plain):
@@ -161,7 +163,7 @@ def tile_picked_forkpullbquadfdif_none_p_kernel(tc, x_words, x_scales, w1, gn, w
             nc.scalar.activation(win_b[t][:, :S], win_a[t][:, :S], ACT.Copy, scale=gm_sb[:, t : t + 1])
         w3_bf = cast_weight("w3", w3_raw)
         z_product(PACK - 1)
-        interleave(z_bf[:], zf[:])
+        interleave(z_bf[:], zf)
 
         def tanh_diff(t):
             diff(d3[t], win_a[t], lists["n3"][:], y_plain[t])
@@ -206,8 +208,8 @@ def tile_picked_forkpullbquadfdif_none_p_kernel(tc, x_words, x_scales, w1, gn, w
             nc.vector.scalar_tensor_tensor(d6[t][:, tok], th[t][:, tok], 1.0, d5[t][:, tok], ALU.add, ALU.mult)
 
         def finish(t, tok=slice(0, S)):
-            nc.vector.scalar_tensor_tensor(zf[:, t, tok], d6[t][:, tok], 0.5, a_plain[t][:, tok], ALU.mult, ALU.add)
-            nc.sync.dma_start(out_rows[:, t, tok], zf[:, t, tok])
+            nc.vector.scalar_tensor_tensor(res[t][:, tok], d6[t][:, tok], 0.5, a_plain[t][:, tok], ALU.mult, ALU.add)
+            nc.sync.dma_start(out_rows[:, t, tok], res[t][:, tok])
 
         gate(0)
         gate(1)

@@ -36,21 +36,19 @@ def tile_picked_forkpullbquadfdif_none_p_kernel(tc, x_words, x_scales, w1, gn, w
             nc.sync.dma_start(lists[name][:], src)
 
         xs_all = sb("xs_all", [P, T], U8)
-        nc.gpsimd.memset(xs_all[:, : 3 * T // 4].bitcast(I32), 0)
-        nc.vector.memset(xs_all[:, 3 * T // 4 :].bitcast(I32), 0)
-        gn_raw = keep.tile([P, PACK], F32, name="gn_raw", tag="gn_then_words", align_bytes=64)
-        nc.sync.dma_start(gn_raw[:], gn.rearrange("(p t) o -> p (t o)", t=PACK))
+        nc.gpsimd.memset(xs_all[:].bitcast(I32), 0)
+        xs_rows = sb("xs_rows", [P, T], U8)
+        for q in range(4):
+            nc.sync.dma_start(xs_rows[q:P:32, :].bitcast(I32), x_scales[0, q:16:4, :].bitcast(I32))
         load_list("offs", offs)
         w1_raw = sb("w1_raw", [P, PACK, H], F32)
         nc.sync.dma_start(w1_raw[:], w1.rearrange("(p j) c -> p j c", j=PACK))
-        for q in range(4):
-            nc.sync.dma_start(xs_all[q:P:32, :].bitcast(I32), x_scales[0, q:16:4, :].bitcast(I32))
-        gn_sb = sb("gn_sb", [P, PACK], F32)
-        nc.vector.tensor_scalar_mul(gn_sb[:], gn_raw[:], 0.75)
-        xw_all = keep.tile([P, T], I32, name="xw_all", tag="gn_then_words", align_bytes=64)
+        xw_all = sb("xw_all", [P, T], I32)
         nc.sync.dma_start(xw_all[:], x_words[0].rearrange("p n t -> p (n t)").bitcast(I32))
         load_list("n1", n1)
         load_list("n2", n2)
+        gn_sb = sb("gn_sb", [P, PACK], F32)
+        nc.sync.dma_start(gn_sb[:], gn.rearrange("(p t) o -> p (t o)", t=PACK))
         gm_sb = sb("gm_sb", [P, PACK], F32)
         load_list("n3", n3)
         nc.sync.dma_start(gm_sb[:], gm.rearrange("(p t) o -> p (t o)", t=PACK))
@@ -70,6 +68,8 @@ def tile_picked_forkpullbquadfdif_none_p_kernel(tc, x_words, x_scales, w1, gn, w
 
         lo_half, hi_half = slice(0, S // 2), slice(S // 2, S)
         xs = sb("xs", [P, S], U8)
+        for q in range(4):
+            nc.vector.tensor_copy(xs_all[32 * q : 32 * q + 4, :].bitcast(I32), xs_rows[32 * q : 32 * q + 4, :].bitcast(I32))
         xw = [sb("xw%d" % h, [P, S // 2], U32) for h in range(2)]
         nc.vector.tensor_copy(xs[:], xs_all[:].indirect(lists["offs"][:]))
 
@@ -79,9 +79,9 @@ def tile_picked_forkpullbquadfdif_none_p_kernel(tc, x_words, x_scales, w1, gn, w
         def by_line(raw):
             return raw[:].rearrange("p j (m t) -> p m j t", t=PACK)
 
-        w1_bf = sb("w1_bf", [P, PACK * H], BF16)
-        nc.scalar.copy(dealt(w1_bf)[:, 0:96], by_line(w1_raw)[:, 0:96])
-        nc.vector.tensor_copy(dealt(w1_bf)[:, 96:128], by_line(w1_raw)[:, 96:128])
+        w1_bf = [sb("w1_bf%d" % u, [P, 2 * H], BF16) for u in range(2)]
+        nc.vector.tensor_copy(w1_bf[0][:].rearrange("p (t m j) -> p m j t", t=2, j=PACK), by_line(w1_raw)[:, :, :, 0:2])
+        nc.scalar.copy(w1_bf[1][:].rearrange("p (t m j) -> p m j t", t=2, j=PACK), by_line(w1_raw)[:, :, :, 2:4])
         w1_codes = sb("w1_codes", [P, H], U32)
         w1_sc = sb("w1_sc", [P, H], U8)
 
@@ -95,7 +95,8 @@ def tile_picked_forkpullbquadfdif_none_p_kernel(tc, x_words, x_scales, w1, gn, w
 
         spare_bank = bank_a[PACK - 1]
 
-        nc.vector.quantize_mx(out=w1_codes[:].bitcast(FP8X4), scales=w1_sc[:], in_=w1_bf[:])
+        nc.vector.quantize_mx(out=w1_codes[:, lo_half].bitcast(FP8X4), scales=w1_sc[:, lo_half], in_=w1_bf[0][:])
+        nc.vector.quantize_mx(out=w1_codes[:, hi_half].bitcast(FP8X4), scales=w1_sc[:, hi_half], in_=w1_bf[1][:])
         nc.vector.tensor_copy(xw[0][:], xw_all[:].bitcast(U32).indirect(lists["offs"][:, 0:16]))
         nc.vector.tensor_copy(xw[1][:], xw_all[:].bitcast(U32).indirect(lists["offs"][:, 16:32]))
         product(bank_yb[0][:, lo_half], w1_codes, w1_sc, 0, xw[0][:], xs[:, lo_half])
@@ -144,9 +145,9 @@ def tile_picked_forkpullbquadfdif_none_p_kernel(tc, x_words, x_scales, w1, gn, w
             nc.vector.quantize_mx(out=codes[:].bitcast(FP8X4), scales=sc[:], in_=src[:])
             return codes, sc
 
-        def interleave(dst, src):
-            nc.scalar.copy(dst.rearrange("p (c i t) -> p c t i", i=4, t=PACK),
-                           src.rearrange("p t (c i) -> p c t i", i=4))
+        def interleave(dst, src, scale):
+            nc.scalar.activation(dst.rearrange("p (c i t) -> p c t i", i=4, t=PACK),
+                                 src.rearrange("p t (c i) -> p c t i", i=4), ACT.Copy, scale=scale)
 
         y_plain = [win_b[t][:, S:] for t in range(PACK)]
         for t in range(PACK):
@@ -163,7 +164,7 @@ def tile_picked_forkpullbquadfdif_none_p_kernel(tc, x_words, x_scales, w1, gn, w
             nc.scalar.activation(win_b[t][:, :S], win_a[t][:, :S], ACT.Copy, scale=gm_sb[:, t : t + 1])
         w3_bf = cast_weight("w3", w3_raw)
         z_product(PACK - 1)
-        interleave(z_bf[:], zf)
+        interleave(z_bf[:], zf, 0.75)
 
         def tanh_diff(t):
             diff(d3[t], win_a[t], lists["n3"][:], y_plain[t])
@@ -185,7 +186,7 @@ def tile_picked_forkpullbquadfdif_none_p_kernel(tc, x_words, x_scales, w1, gn, w
             nc.scalar.copy(win_a[t][:, :S], bank_a[t][:])
             nc.scalar.copy(a_plain[t][:], bank_a[t][:])
         for h in range(2):
-            interleave(z2_bf[:, 2 * S * h : 2 * S * (h + 1)], z2f[h])
+            interleave(z2_bf[:, 2 * S * h : 2 * S * (h + 1)], z2f[h], 1.0)
         for t in range(PACK):
             diff(d5[t], win_a[t], lists["n5"][:], a_plain[t][:])
             if t == 1:

from contextlib import ExitStack

import concourse.mybir as mybir

K, T, S, H, N = 512, 2048, 512, 512, 512
FLOPS = 2 * S * (K * H + 2 * H * N)

F32 = mybir.dt.float32
BF16 = mybir.dt.bfloat16
I32 = mybir.dt.int32
U32 = mybir.dt.uint32
U16 = mybir.dt.uint16
U8 = mybir.dt.uint8
FP8X4 = mybir.dt.float8_e4m3fn_x4
ALU = mybir.AluOpType
ACT = mybir.ActivationFunctionType

P = 128
PACK = 4
WIN = 2 * S


def tile_picked_forkpullbquadfdif_none_p_kernel(tc, x_words, x_scales, w1, gn, w2, gm, w3, offs, n1, n2, n3, n4, n5, n6, out):
    nc = tc.nc
    with ExitStack() as ctx:
        keep = ctx.enter_context(tc.tile_pool(name="keep", bufs=1))
        psum = ctx.enter_context(tc.psum_pool(name="psum", bufs=1))

        def sb(name, shape, dtype):
            return keep.tile(shape, dtype, name=name, align_bytes=64)

        lists = {}

        def load_list(name, src):
            lists[name] = sb("list_" + name, [P, S // 16], U16)
            nc.sync.dma_start(lists[name][:], src)

        xs_all = sb("xs_all", [P, T], U8)
        nc.gpsimd.memset(xs_all[:].bitcast(I32), 0)
        xs_rows = sb("xs_rows", [P, T], U8)
        for q in range(4):
            nc.sync.dma_start(xs_rows[q:P:32, :].bitcast(I32), x_scales[0, q:16:4, :].bitcast(I32))
        load_list("offs", offs)
        w1_raw = sb("w1_raw", [P, PACK, H], F32)
        nc.sync.dma_start(w1_raw[:], w1.rearrange("(p j) c -> p j c", j=PACK))
        xw_all = sb("xw_all", [P, T], I32)
        nc.sync.dma_start(xw_all[:], x_words[0].rearrange("p n t -> p (n t)").bitcast(I32))
        load_list("n1", n1)
        load_list("n2", n2)
        gn_sb = sb("gn_sb", [P, PACK], F32)
        nc.sync.dma_start(gn_sb[:], gn.rearrange("(p t) o -> p (t o)", t=PACK))
        gm_sb = sb("gm_sb", [P, PACK], F32)
        load_list("n3", n3)
        nc.sync.dma_start(gm_sb[:], gm.rearrange("(p t) o -> p (t o)", t=PACK))
        w2_raw = sb("w2_raw", [P, PACK, N], F32)
        nc.sync.dma_start(w2_raw[:], w2.rearrange("(p j) c -> p j c", j=PACK))
        w3_raw = sb("w3_raw", [P, PACK, N], F32)
        nc.sync.dma_start(w3_raw[:], w3.rearrange("(p j) c -> p j c", j=PACK))
        load_list("n4", n4)
        load_list("n5", n5)
        load_list("n6", n6)


        win_a = [sb("win_a%d" % t, [P, WIN], F32) for t in range(PACK)]
        win_b = [sb("win_b%d" % t, [P, WIN], F32) for t in range(PACK)]
        for t in range(PACK):
            nc.vector.memset(win_a[t][:, S:], 0.0)

        lo_half, hi_half = slice(0, S // 2), slice(S // 2, S)
        xs = sb("xs", [P, S], U8)
        for q in range(4):
            nc.vector.tensor_copy(xs_all[32 * q : 32 * q + 4, :].bitcast(I32), xs_rows[32 * q : 32 * q + 4, :].bitcast(I32))
        xw = [sb("xw%d" % h, [P, S // 2], U32) for h in range(2)]
        nc.vector.tensor_copy(xs[:], xs_all[:].indirect(lists["offs"][:]))

        def dealt(grouped):
            return grouped[:].rearrange("p (t m j) -> p m j t", t=PACK, j=PACK)

        def by_line(raw):
            return raw[:].rearrange("p j (m t) -> p m j t", t=PACK)

        w1_bf = [sb("w1_bf%d" % u, [P, 2 * H], BF16) for u in range(2)]
        nc.vector.tensor_copy(w1_bf[0][:].rearrange("p (t m j) -> p m j t", t=2, j=PACK), by_line(w1_raw)[:, :, :, 0:2])
        nc.scalar.copy(w1_bf[1][:].rearrange("p (t m j) -> p m j t", t=2, j=PACK), by_line(w1_raw)[:, :, :, 2:4])
        w1_codes = sb("w1_codes", [P, H], U32)
        w1_sc = sb("w1_sc", [P, H], U8)

        bank_yb = [psum.tile([P, S], F32, name="bank_yb%d" % t) for t in range(PACK)]
        bank_a = [psum.tile([P, S], F32, name="bank_a%d" % t) for t in range(PACK)]

        def product(dst, w_codes, w_sc, t, codes, sc):
            cols = slice(t * P, (t + 1) * P)
            nc.tensor.matmul_mx(out=dst, lhsT=w_codes[:, cols].bitcast(FP8X4), lhsT_scale=w_sc[:, cols],
                                rhs=codes.bitcast(FP8X4), rhs_scale=sc, start=True, stop=True)

        spare_bank = bank_a[PACK - 1]

        nc.vector.quantize_mx(out=w1_codes[:, lo_half].bitcast(FP8X4), scales=w1_sc[:, lo_half], in_=w1_bf[0][:])
        nc.vector.quantize_mx(out=w1_codes[:, hi_half].bitcast(FP8X4), scales=w1_sc[:, hi_half], in_=w1_bf[1][:])
        nc.vector.tensor_copy(xw[0][:], xw_all[:].bitcast(U32).indirect(lists["offs"][:, 0:16]))
        nc.vector.tensor_copy(xw[1][:], xw_all[:].bitcast(U32).indirect(lists["offs"][:, 16:32]))
        product(bank_yb[0][:, lo_half], w1_codes, w1_sc, 0, xw[0][:], xs[:, lo_half])
        product(spare_bank[:, hi_half], w1_codes, w1_sc, 0, xw[1][:], xs[:, hi_half])
        for t in range(1, PACK):
            product(bank_yb[t][:, lo_half], w1_codes, w1_sc, t, xw[0][:], xs[:, lo_half])
            product(bank_yb[t][:, hi_half], w1_codes, w1_sc, t, xw[1][:], xs[:, hi_half])

        nc.scalar.copy(win_a[0][:, lo_half], bank_yb[0][:, lo_half])
        nc.vector.tensor_copy(win_b[0][:, S : S + S // 2], bank_yb[0][:, lo_half])
        nc.scalar.copy(win_a[0][:, hi_half], spare_bank[:, hi_half])
        nc.scalar.copy(win_b[0][:, S + S // 2 :], spare_bank[:, hi_half])
        for t in range(1, PACK):
            nc.scalar.copy(win_a[t][:, :S], bank_yb[t][:])
            nc.scalar.copy(win_b[t][:, S:], bank_yb[t][:])

        d1 = [sb("d1_%d" % t, [P, S], F32) for t in range(PACK)]
        d2 = [sb("d2_%d" % t, [P, S], F32) for t in range(PACK)]
        z_bf = sb("z_bf", [P, PACK * S], BF16)
        z2_bf = sb("z2_bf", [P, PACK * S], BF16)
        zf_flat = sb("zf", [P, PACK * S], F32)
        zf = zf_flat[:].rearrange("p (t c) -> p t c", t=PACK)
        res = [sb("res%d" % t, [P, S], F32) for t in range(PACK)]
        d3 = [d1[2][:], d1[3][:], d2[3][:], zf_flat[:, S // 2 : 3 * S // 2]]
        d5 = [d1[0][:], d1[1][:], zf_flat[:, :S], zf_flat[:, S : 2 * S]]
        d6 = [sb("d6_%d" % t, [P, S], F32) for t in range(PACK)]
        th = [sb("th_%d" % t, [P, S], F32) for t in range(PACK)]
        z2f_lo = sb("z2f_lo", [P, PACK * S // 2], F32)
        z2f = [z2f_lo[:].rearrange("p (t c) -> p t c", t=PACK), zf_flat[:, : 2 * S].rearrange("p (t c) -> p t c", t=PACK)]
        halves = [lo_half, hi_half]

        def diff(dst, win, offsets, plain):
            nc.vector.tensor_tensor(dst, win[:].indirect(offsets), plain, ALU.subtract)

        def z_product(t):
            nc.vector.scalar_tensor_tensor(zf[:, t, :], d1[t][:], gn_sb[:, t : t + 1], d2[t][:], ALU.mult, ALU.mult)

        def cast_weight(name, raw):
            w_bf = sb(name + "_bf", [P, PACK * N], BF16)
            nc.scalar.copy(dealt(w_bf), by_line(raw))
            return w_bf

        def quantise(name, src):
            codes = sb(name + "_codes", [P, S], U32)
            sc = sb(name + "_sc", [P, S], U8)
            nc.vector.quantize_mx(out=codes[:].bitcast(FP8X4), scales=sc[:], in_=src[:])
            return codes, sc

        def interleave(dst, src, scale):
            nc.scalar.activation(dst.rearrange("p (c i t) -> p c t i", i=4, t=PACK),
                                 src.rearrange("p t (c i) -> p c t i", i=4), ACT.Copy, scale=scale)

        y_plain = [win_b[t][:, S:] for t in range(PACK)]
        for t in range(PACK):
            if t == 0:
                diff(d1[0][:, lo_half], win_a[0], lists["n1"][:, 0:16], y_plain[0][:, lo_half])
                diff(d1[0][:, hi_half], win_a[0], lists["n1"][:, 16:32], y_plain[0][:, hi_half])
            else:
                diff(d1[t][:], win_a[t], lists["n1"][:], y_plain[t])
                z_product(t - 1)
            diff(d2[t][:], win_a[t], lists["n2"][:], y_plain[t])
        w2_bf = cast_weight("w2", w2_raw)
        w2_codes, w2_sc = quantise("w2", w2_bf)
        for t in range(PACK):
            nc.scalar.activation(win_b[t][:, :S], win_a[t][:, :S], ACT.Copy, scale=gm_sb[:, t : t + 1])
        w3_bf = cast_weight("w3", w3_raw)
        z_product(PACK - 1)
        interleave(z_bf[:], zf, 0.75)

        def tanh_diff(t):
            diff(d3[t], win_a[t], lists["n3"][:], y_plain[t])
            nc.scalar.activation(th[t][:], d3[t], ACT.Tanh)

        tanh_diff(0)
        tanh_diff(1)
        tanh_diff(2)
        z_codes, z_sc = quantise("z", z_bf)
        tanh_diff(3)
        w3_codes, w3_sc = quantise("w3", w3_bf)
        a_plain = [sb("a_plain%d" % t, [P, S], F32) for t in range(PACK)]
        for t in range(PACK):
            product(bank_a[t][:], w2_codes, w2_sc, t, z_codes[:], z_sc[:])
        for h in range(2):
            for t in range(PACK):
                nc.vector.tensor_tensor(z2f[h][:, t, :], win_b[t][:].indirect(lists["n4"][:, 16 * h : 16 * h + 16]), th[t][:, halves[h]], ALU.mult)
        for t in range(PACK):
            nc.scalar.copy(win_a[t][:, :S], bank_a[t][:])
            nc.scalar.copy(a_plain[t][:], bank_a[t][:])
        for h in range(2):
            interleave(z2_bf[:, 2 * S * h : 2 * S * (h + 1)], z2f[h], 1.0)
        for t in range(PACK):
            diff(d5[t], win_a[t], lists["n5"][:], a_plain[t][:])
            if t == 1:
                z2_codes, z2_sc = quantise("z2", z2_bf)
        for t in range(PACK):
            product(bank_yb[t][:], w3_codes, w3_sc, t, z2_codes[:], z2_sc[:])
        b_plain = [sb("b_plain%d" % t, [P, S], F32) for t in range(PACK)]
        for t in range(PACK):
            nc.scalar.copy(win_b[t][:, :S], bank_yb[t][:])
            nc.scalar.copy(b_plain[t][:], bank_yb[t][:])


        out_rows = out.rearrange("(p t) j -> p t j", t=PACK)

        def gate(t):
            diff(d6[t][:], win_b[t], lists["n6"][:], b_plain[t][:])
            nc.scalar.activation(th[t][:], d6[t][:], ACT.Tanh, scale=0.5)

        def pull(t, tok=slice(0, S)):
            nc.vector.scalar_tensor_tensor(d6[t][:, tok], th[t][:, tok], 1.0, d5[t][:, tok], ALU.add, ALU.mult)

        def finish(t, tok=slice(0, S)):
            nc.vector.scalar_tensor_tensor(res[t][:, tok], d6[t][:, tok], 0.5, a_plain[t][:, tok], ALU.mult, ALU.add)
            nc.sync.dma_start(out_rows[:, t, tok], res[t][:, tok])

        gate(0)
        gate(1)
        pull(0)
        gate(2)
        finish(0)
        pull(1)
        gate(3)
        finish(1)
        pull(2)
        pull(3, lo_half)
        finish(2)
        pull(3, hi_half)
        finish(3, lo_half)
        finish(3, hi_half)
